import numpy as np
import ml_dtypes


def mxq(x, axis, fmt="e4m3"):
    dtype, down = {"e4m3": (ml_dtypes.float8_e4m3fn, 7), "e5m2": (ml_dtypes.float8_e5m2, 14)}[fmt]
    v = np.moveaxis(np.asarray(x, np.float32).astype(ml_dtypes.bfloat16).astype(np.float64), axis, -1)
    blocks = v.reshape(v.shape[:-1] + (-1, 32))
    amax = np.abs(blocks).max(-1, keepdims=True)
    byte = np.maximum(np.where(amax > 0, np.frexp(amax)[1] - 1 + 127, 0) - down, 1)
    scale = np.exp2(byte - 127.0)
    codes = (blocks / scale).astype(np.float32).astype(dtype).astype(np.float64)
    return np.moveaxis((codes * scale).reshape(v.shape), -1, axis)


WIDE = False


def mx_kscale(k):
    if not WIDE:
        return np.ones(k)
    levels = np.array([10, -10, 5, -5, 0])
    if k % 512:
        return np.exp2(np.random.permutation(np.resize(levels, k // 32))).repeat(32)
    a = np.empty((k // 512, 16))
    for p in range(k // 512):
        a[p, :8] = np.random.permutation(np.resize(levels, 8))
        for g in range(8):
            far = levels[np.abs(levels - a[p, g]) >= 10]
            a[p, g + 8] = far[np.random.randint(len(far))]
    return np.exp2(a.ravel()).repeat(32)


def f64(x):
    return np.asarray(x).astype(np.float64)


def striped(idx):
    return np.tile(idx.reshape(-1, 16).T, (8, 1)).astype(np.uint16)


def unstriped(offs):
    return offs[:16].T.reshape(-1).astype(np.int64)

def planes(y):
    n, m = y.shape
    v = y.astype(np.float32).astype(ml_dtypes.bfloat16).astype(np.float64).reshape(n // 32, 32, m)
    top = np.abs(v).max(1)
    byte = np.clip(np.where(top > 0, np.frexp(top)[1] - 1 + 127 - 7, 1), 1, 254)
    codes = (v * np.exp2(127.0 - byte)[:, None, :]).reshape(n, m).astype(np.float32).astype(ml_dtypes.float8_e4m3fn).view(np.uint8)
    words = codes.reshape(n // 512, 128, 4, m).transpose(0, 1, 3, 2)
    return np.ascontiguousarray(words), np.ascontiguousarray(byte.astype(np.uint8).reshape(n // 512, 16, m))


K, T, S, N = 512, 1024, 512, 512
P = 2 ** 7


def setup_inputs():
    n = np.random.standard_normal
    s = mx_kscale(K)[:, None]
    return {
        "xT": (n((K, T)) * s).astype(np.float32),
        "mean": np.tile(0.3 * np.random.standard_normal(T), (P, 1)).astype(np.float32),
        "inv": np.tile(np.random.uniform(0.5, 2.0, T), (P, 1)).astype(np.float32),
        "gsum": n((N, 1)).astype(np.float32),
        "b": (0.3 * n((N, 1))).astype(np.float32),
        "w1": (n((K, N)) / np.sqrt(K) / s).astype(np.float32),
        "offs": striped(np.random.permutation(T)[:S]),
    }


def reference(xT, mean, inv, gsum, b, w1, offs):
    xq = mxq(f64(xT)[:, unstriped(offs)], 0, "e4m3")
    y = mxq(f64(w1), 0, "e4m3").T @ xq
    mg = f64(mean)[:1][:, unstriped(offs)]
    ig = f64(inv)[:1][:, unstriped(offs)]
    out_0 = (y - (f64(gsum) * mg)) * ig + f64(b)
    return (out_0,) + planes(out_0)

@@ -1,0 +1,180 @@
+from contextlib import ExitStack
+
+import concourse.mybir as mybir
+from concourse.masks import make_identity
+
+K, T, S, N = 512, 1024, 512, 512
+FLOPS = 2 * K * S * N
+
+F32 = mybir.dt.float32
+BF16 = mybir.dt.bfloat16
+I32 = mybir.dt.int32
+U32 = mybir.dt.uint32
+U16 = mybir.dt.uint16
+U8 = mybir.dt.uint8
+FP8X4 = mybir.dt.float8_e4m3fn_x4
+MULT = mybir.AluOpType.mult
+ADD = mybir.AluOpType.add
+COPY = mybir.ActivationFunctionType.Copy
+IDENTITY = mybir.ActivationFunctionType.Identity
+
+P = 128
+PACK = 4
+TILES = S // P
+HALF = N // 2
+
+
+def weave(copy, dst, src):
+    copy(
+        out=dst.rearrange("p (c i) t -> p c t i", i=4),
+        in_=src.rearrange("p t (c i) -> p c t i", i=4),
+    )
+
+
+def quantize(nc, codes, scales, woven):
+    nc.vector.quantize_mx(out=codes.bitcast(FP8X4), scales=scales, in_=woven.rearrange("p c t -> p (c t)"))
+
+
+def tile_picked_lnfold_none_lo_kernel(tc, xT, mean, inv, gsum, b, w1, offs, out_0, out_1, out_2):
+    nc = tc.nc
+    with ExitStack() as ctx:
+        sb = ctx.enter_context(tc.tile_pool(name="sb", bufs=1))
+        ps = ctx.enter_context(tc.psum_pool(name="ps", bufs=1))
+
+        lists = sb.tile([P, S // 16], U16, name="lists")
+        nc.sync.dma_start(lists[:], offs)
+        stats = sb.tile([P, T], F32, name="stats")
+        nc.scalar.dma_start(out=stats[0:16, :], in_=mean[0:16, :])
+        nc.sync.dma_start(out=stats[16:32, :], in_=inv[0:16, :])
+        g_col = sb.tile([P, PACK], F32, name="g_col")
+        b_col = sb.tile([P, PACK], F32, name="b_col")
+        nc.scalar.dma_start(out=g_col[:], in_=gsum.rearrange("(p t) o -> p (t o)", t=PACK))
+        x_rows = xT.rearrange("(p t) c -> p t c", t=PACK)
+        x_raw = [sb.tile([P, T], F32, name=f"x_raw{t}", align_bytes=64) for t in range(PACK)]
+        for t in (0, 2, 1, 3):
+            nc.sync.dma_start(out=x_raw[t][:], in_=x_rows[:, t, :])
+        w_rows = w1.rearrange("(p t) m -> p t m", t=PACK)
+        w_raw = [sb.tile([P, PACK, HALF], F32, name=f"w_raw{h}") for h in range(2)]
+        for h in range(2):
+            nc.sync.dma_start(out=w_raw[h][:], in_=w_rows[:, :, h * HALF : (h + 1) * HALF])
+        nc.sync.dma_start(out=b_col[:], in_=b.rearrange("(p t) o -> p (t o)", t=PACK))
+
+        nc.gpsimd.memset(stats[64:128, 0:128], 0.0)
+        nc.gpsimd.memset(stats[64:128, 128:896], 0.0)
+        nc.vector.memset(stats[32:64, :], 0.0)
+        nc.scalar.copy(out=stats[64:128, 896:1024], in_=stats[64:128, 0:128])
+        ident = sb.tile([P, P], F32, name="ident")
+        make_identity(nc, ident[:])
+
+        x_planes = sb.tile([P, PACK * S], BF16, name="x_planes", align_bytes=64)
+        x_picked = x_planes[:].rearrange("p (t c) -> p t c", t=PACK)
+        picked = x_planes[:, 2 * S : 4 * S].bitcast(F32)
+        nc.vector.tensor_copy(out=picked, in_=stats[:].indirect(lists[:]))
+
+        g_bank = ps.tile([P, PACK, P], F32, name="g_bank", tag="y0")
+        for t in range(PACK):
+            nc.tensor.transpose(g_bank[:, t, :], g_col[:, t : t + 1].to_broadcast([P, P]), ident[:])
+        stat_bank = ps.tile([P, TILES, P], F32, name="stat_bank", tag="y1")
+        for i in range(TILES):
+            nc.tensor.transpose(stat_bank[:, i, :], picked[:, i * P : (i + 1) * P], ident[:])
+
+        nc.scalar.activation(out=x_picked[:, 0, :], in_=x_raw[0][:].indirect(lists[:]), func=COPY)
+        g_rows = sb.tile([P, PACK, P], F32, name="g_rows")
+        nc.vector.tensor_copy(out=g_rows[:], in_=g_bank[:])
+        inv_col = sb.tile([P, TILES], F32, name="inv_col")
+        nc.vector.tensor_copy(out=inv_col[:], in_=stat_bank[:, :, 16])
+        mean_col = picked[:, S // 2 - 2 : S // 2 + 2]
+        nc.vector.tensor_copy(out=mean_col, in_=stat_bank[:, :, 0])
+        shift_col = sb.tile([P, TILES], F32, name="shift_col")
+        nc.vector.scalar_tensor_tensor(
+            out=shift_col[:], in0=mean_col, scalar=-1.0, in1=inv_col[:], op0=MULT, op1=MULT
+        )
+        nc.scalar.activation(out=x_picked[:, 1, :], in_=x_raw[1][:].indirect(lists[:]), func=COPY)
+
+        out_banks = [ps.tile([P, PACK, P], F32, name=f"out_bank{i}") for i in range(TILES)]
+        for i in range(TILES):
+            shift = sb.tile([P, PACK, P], F32, name=f"shift{i}", align_bytes=64)
+            nc.gpsimd.tensor_scalar(
+                out=shift[:], in0=g_rows[:], scalar1=shift_col[:, i : i + 1], scalar2=0.0, op0=MULT, op1=ADD
+            )
+            for t in range(PACK):
+                nc.tensor.matmul(
+                    out_banks[i][:, t, :], lhsT=shift[:, t, :], rhs=ident[:], is_transpose=True,
+                    start=(t == 0), stop=False,
+                )
+
+        nc.vector.tensor_copy(out=x_picked[:, 2, :], in_=x_raw[2][:].indirect(lists[:]))
+        nc.vector.tensor_copy(out=x_picked[:, 3, 0:128], in_=x_raw[3][:].indirect(lists[:, 0:8]))
+        nc.scalar.activation(out=x_picked[:, 3, 128:256], in_=x_raw[3][:].indirect(lists[:, 8:16]), func=COPY)
+        nc.scalar.activation(out=x_picked[:, 3, 256:512], in_=x_raw[3][:].indirect(lists[:, 16:32]), func=COPY)
+
+        x_woven = sb.tile([P, S, PACK], BF16, name="x_woven", align_bytes=64)
+        x_codes = sb.tile([P, S], U32, name="x_codes", align_bytes=64)
+        x_scales = sb.tile([P, S], U8, name="x_scales", align_bytes=64)
+        weave(nc.vector.tensor_copy, x_woven[:, 0:128, :], x_picked[:, :, 0:128])
+        weave(nc.vector.tensor_copy, x_woven[:, 128:256, :], x_picked[:, :, 128:256])
+        weave(nc.vector.tensor_copy, x_woven[:, 256:512, :], x_picked[:, :, 256:512])
+        w_woven = [sb.tile([P, HALF, PACK], BF16, name=f"w_woven{h}", tag=("x_raw3", "x_woven")[h], align_bytes=64) for h in range(2)]
+        w_codes = [sb.tile([P, HALF], U32, name=f"w_codes{h}", tag=f"shift{3 - h}", align_bytes=64) for h in range(2)]
+        w_scales = [sb.tile([P, HALF], U8, name=f"w_scales{h}", align_bytes=64) for h in range(2)]
+        weave(nc.scalar.copy, w_woven[0][:], w_raw[0][:])
+        for u in range(2):
+            cols = slice(u * 256, (u + 1) * 256)
+            quantize(nc, x_codes[:, cols], x_scales[:, cols], x_woven[:, cols, :])
+        quantize(nc, w_codes[0][:], w_scales[0][:], w_woven[0][:])
+        weave(nc.vector.tensor_copy, w_woven[1][:, 0:160, :], w_raw[1][:, :, 0:160])
+        weave(nc.scalar.copy, w_woven[1][:, 160:256, :], w_raw[1][:, :, 160:256])
+        quantize(nc, w_codes[1][:], w_scales[1][:], w_woven[1][:])
+
+        y_banks = [ps.tile([P, N], F32, name=f"y_bank{i}", tag=f"y{i}") for i in range(TILES)]
+        scaled = [sb.tile([P, PACK, P], F32, name=f"scaled{i}") for i in range(TILES)]
+        for h in range(2):
+            for i in range(TILES):
+                toks = slice(i * P, (i + 1) * P)
+                y_half = y_banks[i][:, h * HALF : (h + 1) * HALF]
+                nc.tensor.matmul_mx(
+                    out=y_half,
+                    lhsT=x_codes[:, toks].bitcast(FP8X4),
+                    lhsT_scale=x_scales[:, toks],
+                    rhs=w_codes[h][:].bitcast(FP8X4),
+                    rhs_scale=w_scales[h][:],
+                    start=True,
+                    stop=True,
+                )
+                dealt = y_half.rearrange("j (p t) -> j t p", t=PACK)
+                target = scaled[i][:, :, h * 64 : (h + 1) * 64]
+                if h == 1 and i % 2 == 0:
+                    nc.vector.tensor_scalar_mul(target, dealt, inv_col[:, i : i + 1])
+                else:
+                    nc.scalar.activation(out=target, in_=dealt, func=COPY, scale=inv_col[:, i : i + 1])
+
+        out_rows = out_0.rearrange("(p t) j -> p t j", t=PACK)
+        out_words = out_1[0].rearrange("p j r -> p (j r)").bitcast(I32)
+        o_woven = sb.tile([P, S, PACK], BF16, name="o_woven", align_bytes=64)
+        o_codes = sb.tile([P, S], U32, name="o_codes", align_bytes=64)
+        o_scales = sb.tile([P, S], U8, name="o_scales", align_bytes=64)
+        for i in range(TILES):
+            toks = slice(i * P, (i + 1) * P)
+            for t in range(PACK):
+                nc.tensor.matmul(
+                    out_banks[i][:, t, :], lhsT=scaled[i][:, t, :], rhs=ident[:], is_transpose=True,
+                    start=False, stop=(t == PACK - 1),
+                )
+            result = sb.tile([P, PACK, P], F32, name=f"result{i}")
+            for t in range(PACK):
+                if i == 1:
+                    nc.vector.tensor_scalar_add(result[:, t, :], out_banks[i][:, t, :], b_col[:, t : t + 1])
+                else:
+                    nc.scalar.activation(
+                        out=result[:, t, :], in_=out_banks[i][:, t, :], func=IDENTITY, bias=b_col[:, t : t + 1]
+                    )
+            nc.sync.dma_start(out=out_rows[:, :, toks], in_=result[:])
+            weave(nc.vector.tensor_copy, o_woven[:, toks, :], result[:])
+            if i % 2 == 1:
+                pair = slice((i - 1) * P, (i + 1) * P)
+                quantize(nc, o_codes[:, pair], o_scales[:, pair], o_woven[:, pair, :])
+                nc.sync.dma_start(out=out_words[:, pair], in_=o_codes[:, pair].bitcast(I32))
+        scale_rows = out_2[0].bitcast(I32)
+        for q in range(4):
+            queue = nc.scalar if q % 2 else nc.sync
+            queue.dma_start(out=scale_rows[4 * q : 4 * q + 4, :], in_=o_scales[32 * q : 32 * q + 4, :].bitcast(I32))

@@ -66,10 +66,10 @@ def tile_picked_lnfold_none_lo_kernel(tc, xT, mean, inv, gsum, b, w1, offs, out_
         ident = sb.tile([P, P], F32, name="ident")
         make_identity(nc, ident[:])
 
-        x_planes = sb.tile([P, PACK * S], BF16, name="x_planes", align_bytes=64)
-        x_picked = x_planes[:].rearrange("p (t c) -> p t c", t=PACK)
-        picked = x_planes[:, 2 * S : 4 * S].bitcast(F32)
-        nc.vector.tensor_copy(out=picked, in_=stats[:].indirect(lists[:]))
+        x_planes = sb.tile([P, PACK * S + 896], BF16, name="x_planes", align_bytes=64)
+        x_picked = x_planes[:, 0 : PACK * S].rearrange("p (t c) -> p t c", t=PACK)
+        picked = sb.tile([P, S], F32, name="picked")
+        nc.vector.tensor_copy(out=picked[:], in_=stats[:].indirect(lists[:]))
 
         g_bank = ps.tile([P, PACK, P], F32, name="g_bank", tag="y0")
         for t in range(PACK):
@@ -79,11 +79,11 @@ def tile_picked_lnfold_none_lo_kernel(tc, xT, mean, inv, gsum, b, w1, offs, out_
             nc.tensor.transpose(stat_bank[:, i, :], picked[:, i * P : (i + 1) * P], ident[:])
 
         nc.scalar.activation(out=x_picked[:, 0, :], in_=x_raw[0][:].indirect(lists[:]), func=COPY)
-        g_rows = sb.tile([P, PACK, P], F32, name="g_rows")
-        nc.vector.tensor_copy(out=g_rows[:], in_=g_bank[:])
+        g_rows = x_planes[:, PACK * S - P : PACK * S + 896].bitcast(F32)
+        nc.vector.tensor_copy(out=g_rows, in_=g_bank[:].rearrange("p t m -> p (t m)"))
         inv_col = sb.tile([P, TILES], F32, name="inv_col")
         nc.vector.tensor_copy(out=inv_col[:], in_=stat_bank[:, :, 16])
-        mean_col = picked[:, S // 2 - 2 : S // 2 + 2]
+        mean_col = x_planes[:, 2 * S : 2 * S + 2 * TILES].bitcast(F32)
         nc.vector.tensor_copy(out=mean_col, in_=stat_bank[:, :, 0])
         shift_col = sb.tile([P, TILES], F32, name="shift_col")
         nc.vector.scalar_tensor_tensor(
@@ -91,30 +91,33 @@ def tile_picked_lnfold_none_lo_kernel(tc, xT, mean, inv, gsum, b, w1, offs, out_
         )
         nc.scalar.activation(out=x_picked[:, 1, :], in_=x_raw[1][:].indirect(lists[:]), func=COPY)
 
-        out_banks = [ps.tile([P, PACK, P], F32, name=f"out_bank{i}") for i in range(TILES)]
+        nc.vector.tensor_copy(out=x_picked[:, 2, :], in_=x_raw[2][:].indirect(lists[:]))
+        out_banks = [[ps.tile([P, 2, 2 * P], F32, name=f"out_bank{u}{v}") for v in range(2)] for u in range(2)]
+
+        def out_block(i, t):
+            return out_banks[i // 2][t // 2][:, t % 2, (i % 2) * P : (i % 2 + 1) * P]
+
         for i in range(TILES):
             shift = sb.tile([P, PACK, P], F32, name=f"shift{i}", align_bytes=64)
-            nc.gpsimd.tensor_scalar(
-                out=shift[:], in0=g_rows[:], scalar1=shift_col[:, i : i + 1], scalar2=0.0, op0=MULT, op1=ADD
-            )
+            nc.vector.tensor_scalar_mul(shift[:].rearrange("p t m -> p (t m)"), g_rows, shift_col[:, i : i + 1])
             for t in range(PACK):
                 nc.tensor.matmul(
-                    out_banks[i][:, t, :], lhsT=shift[:, t, :], rhs=ident[:], is_transpose=True,
-                    start=(t == 0), stop=False,
+                    out_block(i, t), lhsT=shift[:, t, :], rhs=ident[:], is_transpose=True,
+                    start=(i % 2 == 0 and t % 2 == 0), stop=False,
                 )
 
-        nc.vector.tensor_copy(out=x_picked[:, 2, :], in_=x_raw[2][:].indirect(lists[:]))
-        nc.vector.tensor_copy(out=x_picked[:, 3, 0:128], in_=x_raw[3][:].indirect(lists[:, 0:8]))
-        nc.scalar.activation(out=x_picked[:, 3, 128:256], in_=x_raw[3][:].indirect(lists[:, 8:16]), func=COPY)
-        nc.scalar.activation(out=x_picked[:, 3, 256:512], in_=x_raw[3][:].indirect(lists[:, 16:32]), func=COPY)
+        nc.vector.tensor_copy(out=x_picked[:, 3, 384:512], in_=x_raw[3][:].indirect(lists[:, 24:32]))
+        for i in range(TILES - 1):
+            nc.scalar.activation(
+                out=x_picked[:, 3, i * P : (i + 1) * P], in_=x_raw[3][:].indirect(lists[:, 8 * i : 8 * i + 8]), func=COPY
+            )
 
         x_woven = sb.tile([P, S, PACK], BF16, name="x_woven", align_bytes=64)
         x_codes = sb.tile([P, S], U32, name="x_codes", align_bytes=64)
         x_scales = sb.tile([P, S], U8, name="x_scales", align_bytes=64)
-        weave(nc.vector.tensor_copy, x_woven[:, 0:128, :], x_picked[:, :, 0:128])
-        weave(nc.vector.tensor_copy, x_woven[:, 128:256, :], x_picked[:, :, 128:256])
-        weave(nc.vector.tensor_copy, x_woven[:, 256:512, :], x_picked[:, :, 256:512])
-        w_woven = [sb.tile([P, HALF, PACK], BF16, name=f"w_woven{h}", tag=("x_raw3", "x_woven")[h], align_bytes=64) for h in range(2)]
+        for i in (0, 3, 1, 2):
+            weave(nc.vector.tensor_copy, x_woven[:, i * P : (i + 1) * P, :], x_picked[:, :, i * P : (i + 1) * P])
+        w_woven = [sb.tile([P, HALF, PACK], BF16, name=f"w_woven{h}", tag=("x_raw3", "x_planes")[h], align_bytes=64) for h in range(2)]
         w_codes = [sb.tile([P, HALF], U32, name=f"w_codes{h}", tag=f"shift{3 - h}", align_bytes=64) for h in range(2)]
         w_scales = [sb.tile([P, HALF], U8, name=f"w_scales{h}", align_bytes=64) for h in range(2)]
         weave(nc.scalar.copy, w_woven[0][:], w_raw[0][:])
@@ -122,18 +125,16 @@ def tile_picked_lnfold_none_lo_kernel(tc, xT, mean, inv, gsum, b, w1, offs, out_
             cols = slice(u * 256, (u + 1) * 256)
             quantize(nc, x_codes[:, cols], x_scales[:, cols], x_woven[:, cols, :])
         quantize(nc, w_codes[0][:], w_scales[0][:], w_woven[0][:])
-        weave(nc.vector.tensor_copy, w_woven[1][:, 0:160, :], w_raw[1][:, :, 0:160])
-        weave(nc.scalar.copy, w_woven[1][:, 160:256, :], w_raw[1][:, :, 160:256])
+        weave(nc.vector.tensor_copy, w_woven[1][:, 0:96, :], w_raw[1][:, :, 0:96])
+        weave(nc.scalar.copy, w_woven[1][:, 96:256, :], w_raw[1][:, :, 96:256])
         quantize(nc, w_codes[1][:], w_scales[1][:], w_woven[1][:])
 
         y_banks = [ps.tile([P, N], F32, name=f"y_bank{i}", tag=f"y{i}") for i in range(TILES)]
-        scaled = [sb.tile([P, PACK, P], F32, name=f"scaled{i}") for i in range(TILES)]
         for h in range(2):
             for i in range(TILES):
                 toks = slice(i * P, (i + 1) * P)
-                y_half = y_banks[i][:, h * HALF : (h + 1) * HALF]
                 nc.tensor.matmul_mx(
-                    out=y_half,
+                    out=y_banks[i][:, h * HALF : (h + 1) * HALF],
                     lhsT=x_codes[:, toks].bitcast(FP8X4),
                     lhsT_scale=x_scales[:, toks],
                     rhs=w_codes[h][:].bitcast(FP8X4),
@@ -141,39 +142,41 @@ def tile_picked_lnfold_none_lo_kernel(tc, xT, mean, inv, gsum, b, w1, offs, out_
                     start=True,
                     stop=True,
                 )
-                dealt = y_half.rearrange("j (p t) -> j t p", t=PACK)
-                target = scaled[i][:, :, h * 64 : (h + 1) * 64]
-                if h == 1 and i % 2 == 0:
-                    nc.vector.tensor_scalar_mul(target, dealt, inv_col[:, i : i + 1])
-                else:
-                    nc.scalar.activation(out=target, in_=dealt, func=COPY, scale=inv_col[:, i : i + 1])
+        scaled = [sb.tile([P, PACK, P], F32, name=f"scaled{i}") for i in range(TILES)]
+        for i in range(TILES):
+            dealt = y_banks[i][:].rearrange("j (p t) -> j t p", t=PACK)
+            if i % 2 == 0:
+                nc.scalar.activation(out=scaled[i][:], in_=dealt, func=COPY, scale=inv_col[:, i : i + 1])
+            else:
+                nc.vector.tensor_scalar_mul(scaled[i][:], dealt, inv_col[:, i : i + 1])
 
         out_rows = out_0.rearrange("(p t) j -> p t j", t=PACK)
         out_words = out_1[0].rearrange("p j r -> p (j r)").bitcast(I32)
         o_woven = sb.tile([P, S, PACK], BF16, name="o_woven", align_bytes=64)
         o_codes = sb.tile([P, S], U32, name="o_codes", align_bytes=64)
         o_scales = sb.tile([P, S], U8, name="o_scales", align_bytes=64)
-        for i in range(TILES):
-            toks = slice(i * P, (i + 1) * P)
-            for t in range(PACK):
-                nc.tensor.matmul(
-                    out_banks[i][:, t, :], lhsT=scaled[i][:, t, :], rhs=ident[:], is_transpose=True,
-                    start=False, stop=(t == PACK - 1),
-                )
-            result = sb.tile([P, PACK, P], F32, name=f"result{i}")
-            for t in range(PACK):
-                if i == 1:
-                    nc.vector.tensor_scalar_add(result[:, t, :], out_banks[i][:, t, :], b_col[:, t : t + 1])
-                else:
-                    nc.scalar.activation(
-                        out=result[:, t, :], in_=out_banks[i][:, t, :], func=IDENTITY, bias=b_col[:, t : t + 1]
+        for u in range(2):
+            pair = slice(u * 2 * P, (u + 1) * 2 * P)
+            for i in (2 * u, 2 * u + 1):
+                for t in range(PACK):
+                    nc.tensor.matmul(
+                        out_block(i, t), lhsT=scaled[i][:, t, :], rhs=ident[:], is_transpose=True,
+                        start=False, stop=(i % 2 == 1 and t % 2 == 1),
                     )
-            nc.sync.dma_start(out=out_rows[:, :, toks], in_=result[:])
-            weave(nc.vector.tensor_copy, o_woven[:, toks, :], result[:])
-            if i % 2 == 1:
-                pair = slice((i - 1) * P, (i + 1) * P)
-                quantize(nc, o_codes[:, pair], o_scales[:, pair], o_woven[:, pair, :])
-                nc.sync.dma_start(out=out_words[:, pair], in_=o_codes[:, pair].bitcast(I32))
+            result = sb.tile([P, PACK, 2 * P], F32, name=f"result{u}")
+            for t in range(PACK):
+                bank = out_banks[u][t // 2][:, t % 2, :]
+                if t < 2:
+                    nc.scalar.activation(out=result[:, t, :], in_=bank, func=IDENTITY, bias=b_col[:, t : t + 1])
+                else:
+                    nc.vector.tensor_scalar_add(result[:, t, :], bank, b_col[:, t : t + 1])
+            for v in range(2):
+                nc.sync.dma_start(out=out_rows[:, 2 * v : 2 * v + 2, pair], in_=result[:, 2 * v : 2 * v + 2, :])
+            woven = o_woven[:, pair, :]
+            weave(nc.vector.tensor_copy, woven[:, 0:160, :], result[:, :, 0:160])
+            weave(nc.scalar.copy, woven[:, 160:256, :], result[:, :, 160:256])
+            quantize(nc, o_codes[:, pair], o_scales[:, pair], woven)
+            nc.sync.dma_start(out=out_words[:, pair], in_=o_codes[:, pair].bitcast(I32))
         scale_rows = out_2[0].bitcast(I32)
         for q in range(4):
             queue = nc.scalar if q % 2 else nc.sync

@@ -46,28 +46,27 @@ def tile_picked_lnfold_none_lo_kernel(tc, xT, mean, inv, gsum, b, w1, offs, out_
         stats = sb.tile([P, T], F32, name="stats")
         nc.scalar.dma_start(out=stats[0:16, :], in_=mean[0:16, :])
         nc.sync.dma_start(out=stats[16:32, :], in_=inv[0:16, :])
-        g_col = sb.tile([P, PACK], F32, name="g_col")
-        b_col = sb.tile([P, PACK], F32, name="b_col")
-        nc.scalar.dma_start(out=g_col[:], in_=gsum.rearrange("(p t) o -> p (t o)", t=PACK))
-        x_rows = xT.rearrange("(p t) c -> p t c", t=PACK)
-        x_raw = [sb.tile([P, T], F32, name=f"x_raw{t}", align_bytes=64) for t in range(PACK)]
-        for t in (0, 2, 1, 3):
-            nc.sync.dma_start(out=x_raw[t][:], in_=x_rows[:, t, :])
-        w_rows = w1.rearrange("(p t) m -> p t m", t=PACK)
-        w_raw = [sb.tile([P, PACK, HALF], F32, name=f"w_raw{h}") for h in range(2)]
-        for h in range(2):
-            nc.sync.dma_start(out=w_raw[h][:], in_=w_rows[:, :, h * HALF : (h + 1) * HALF])
-        nc.sync.dma_start(out=b_col[:], in_=b.rearrange("(p t) o -> p (t o)", t=PACK))
-
         nc.gpsimd.memset(stats[64:128, 0:128], 0.0)
         nc.gpsimd.memset(stats[64:128, 128:896], 0.0)
         nc.vector.memset(stats[32:64, :], 0.0)
         nc.scalar.copy(out=stats[64:128, 896:1024], in_=stats[64:128, 0:128])
+        g_col = sb.tile([P, PACK], F32, name="g_col")
+        b_col = sb.tile([P, PACK], F32, name="b_col")
+        nc.scalar.dma_start(out=g_col[:], in_=gsum.rearrange("(p t) o -> p (t o)", t=PACK))
+        w_rows = w1.rearrange("(p t) m -> p t m", t=PACK)
+        w_raw = [sb.tile([P, PACK, HALF], F32, name=f"w_raw{h}") for h in range(2)]
+        nc.sync.dma_start(out=w_raw[0][:], in_=w_rows[:, :, 0:HALF])
+        nc.sync.dma_start(out=w_raw[1][:], in_=w_rows[:, :, HALF:N])
+        x_rows = xT.rearrange("(p t) c -> p t c", t=PACK)
+        x_raw = [sb.tile([P, T], F32, name=f"x_raw{t}") for t in range(PACK)]
+        for t in range(PACK):
+            nc.sync.dma_start(out=x_raw[t][:], in_=x_rows[:, t, :])
+        nc.sync.dma_start(out=b_col[:], in_=b.rearrange("(p t) o -> p (t o)", t=PACK))
         ident = sb.tile([P, P], F32, name="ident")
         make_identity(nc, ident[:])
 
-        x_planes = sb.tile([P, PACK * S + 896], BF16, name="x_planes", align_bytes=64)
-        x_picked = x_planes[:, 0 : PACK * S].rearrange("p (t c) -> p t c", t=PACK)
+        x_planes = sb.tile([P, PACK * S], BF16, name="x_planes", align_bytes=64)
+        x_picked = x_planes[:].rearrange("p (t c) -> p t c", t=PACK)
         picked = sb.tile([P, S], F32, name="picked")
         nc.vector.tensor_copy(out=picked[:], in_=stats[:].indirect(lists[:]))
 
@@ -78,20 +77,23 @@ def tile_picked_lnfold_none_lo_kernel(tc, xT, mean, inv, gsum, b, w1, offs, out_
         for i in range(TILES):
             nc.tensor.transpose(stat_bank[:, i, :], picked[:, i * P : (i + 1) * P], ident[:])
 
-        nc.scalar.activation(out=x_picked[:, 0, :], in_=x_raw[0][:].indirect(lists[:]), func=COPY)
-        g_rows = x_planes[:, PACK * S - P : PACK * S + 896].bitcast(F32)
+        g_rows = x_planes[:, 2 * S : 4 * S].bitcast(F32)
         nc.vector.tensor_copy(out=g_rows, in_=g_bank[:].rearrange("p t m -> p (t m)"))
         inv_col = sb.tile([P, TILES], F32, name="inv_col")
         nc.vector.tensor_copy(out=inv_col[:], in_=stat_bank[:, :, 16])
-        mean_col = x_planes[:, 2 * S : 2 * S + 2 * TILES].bitcast(F32)
-        nc.vector.tensor_copy(out=mean_col, in_=stat_bank[:, :, 0])
         shift_col = sb.tile([P, TILES], F32, name="shift_col")
         nc.vector.scalar_tensor_tensor(
-            out=shift_col[:], in0=mean_col, scalar=-1.0, in1=inv_col[:], op0=MULT, op1=MULT
+            out=shift_col[:], in0=stat_bank[:, :, 0], scalar=-1.0, in1=inv_col[:], op0=MULT, op1=MULT
         )
-        nc.scalar.activation(out=x_picked[:, 1, :], in_=x_raw[1][:].indirect(lists[:]), func=COPY)
 
-        nc.vector.tensor_copy(out=x_picked[:, 2, :], in_=x_raw[2][:].indirect(lists[:]))
+        w_codes = sb.tile([P, N], U32, name="w_codes", align_bytes=64)
+        w_scales = sb.tile([P, N], U8, name="w_scales", align_bytes=64)
+        for h in range(2):
+            cols = slice(h * HALF, (h + 1) * HALF)
+            w_woven = sb.tile([P, HALF, PACK], BF16, name=f"w_woven{h}", tag=f"shift{2 + h}", align_bytes=64)
+            weave(nc.scalar.copy, w_woven[:], w_raw[h][:])
+            quantize(nc, w_codes[:, cols], w_scales[:, cols], w_woven[:])
+
         out_banks = [[ps.tile([P, 2, 2 * P], F32, name=f"out_bank{u}{v}") for v in range(2)] for u in range(2)]
 
         def out_block(i, t):
@@ -106,8 +108,11 @@ def tile_picked_lnfold_none_lo_kernel(tc, xT, mean, inv, gsum, b, w1, offs, out_
                     start=(i % 2 == 0 and t % 2 == 0), stop=False,
                 )
 
-        nc.vector.tensor_copy(out=x_picked[:, 3, 384:512], in_=x_raw[3][:].indirect(lists[:, 24:32]))
-        for i in range(TILES - 1):
+        for t in range(2):
+            nc.scalar.activation(out=x_picked[:, t, :], in_=x_raw[t][:].indirect(lists[:]), func=COPY)
+        nc.vector.tensor_copy(out=x_picked[:, 2, :], in_=x_raw[2][:].indirect(lists[:]))
+        nc.vector.tensor_copy(out=x_picked[:, 3, 0:P], in_=x_raw[3][:].indirect(lists[:, 0:8]))
+        for i in range(1, TILES):
             nc.scalar.activation(
                 out=x_picked[:, 3, i * P : (i + 1) * P], in_=x_raw[3][:].indirect(lists[:, 8 * i : 8 * i + 8]), func=COPY
             )
@@ -115,33 +120,27 @@ def tile_picked_lnfold_none_lo_kernel(tc, xT, mean, inv, gsum, b, w1, offs, out_
         x_woven = sb.tile([P, S, PACK], BF16, name="x_woven", align_bytes=64)
         x_codes = sb.tile([P, S], U32, name="x_codes", align_bytes=64)
         x_scales = sb.tile([P, S], U8, name="x_scales", align_bytes=64)
-        for i in (0, 3, 1, 2):
-            weave(nc.vector.tensor_copy, x_woven[:, i * P : (i + 1) * P, :], x_picked[:, :, i * P : (i + 1) * P])
-        w_woven = [sb.tile([P, HALF, PACK], BF16, name=f"w_woven{h}", tag=("x_raw3", "x_planes")[h], align_bytes=64) for h in range(2)]
-        w_codes = [sb.tile([P, HALF], U32, name=f"w_codes{h}", tag=f"shift{3 - h}", align_bytes=64) for h in range(2)]
-        w_scales = [sb.tile([P, HALF], U8, name=f"w_scales{h}", align_bytes=64) for h in range(2)]
-        weave(nc.scalar.copy, w_woven[0][:], w_raw[0][:])
         for u in range(2):
-            cols = slice(u * 256, (u + 1) * 256)
-            quantize(nc, x_codes[:, cols], x_scales[:, cols], x_woven[:, cols, :])
-        quantize(nc, w_codes[0][:], w_scales[0][:], w_woven[0][:])
-        weave(nc.vector.tensor_copy, w_woven[1][:, 0:96, :], w_raw[1][:, :, 0:96])
-        weave(nc.scalar.copy, w_woven[1][:, 96:256, :], w_raw[1][:, :, 96:256])
-        quantize(nc, w_codes[1][:], w_scales[1][:], w_woven[1][:])
+            for i in (2 * u, 2 * u + 1):
+                toks = slice(i * P, (i + 1) * P)
+                copy = nc.scalar.copy if i == TILES - 1 else nc.vector.tensor_copy
+                weave(copy, x_woven[:, toks, :], x_picked[:, :, toks])
+            for i in (2 * u, 2 * u + 1):
+                toks = slice(i * P, (i + 1) * P)
+                quantize(nc, x_codes[:, toks], x_scales[:, toks], x_woven[:, toks, :])
 
         y_banks = [ps.tile([P, N], F32, name=f"y_bank{i}", tag=f"y{i}") for i in range(TILES)]
-        for h in range(2):
-            for i in range(TILES):
-                toks = slice(i * P, (i + 1) * P)
-                nc.tensor.matmul_mx(
-                    out=y_banks[i][:, h * HALF : (h + 1) * HALF],
-                    lhsT=x_codes[:, toks].bitcast(FP8X4),
-                    lhsT_scale=x_scales[:, toks],
-                    rhs=w_codes[h][:].bitcast(FP8X4),
-                    rhs_scale=w_scales[h][:],
-                    start=True,
-                    stop=True,
-                )
+        for i in range(TILES):
+            toks = slice(i * P, (i + 1) * P)
+            nc.tensor.matmul_mx(
+                out=y_banks[i][:],
+                lhsT=x_codes[:, toks].bitcast(FP8X4),
+                lhsT_scale=x_scales[:, toks],
+                rhs=w_codes[:].bitcast(FP8X4),
+                rhs_scale=w_scales[:],
+                start=True,
+                stop=True,
+            )
         scaled = [sb.tile([P, PACK, P], F32, name=f"scaled{i}") for i in range(TILES)]
         for i in range(TILES):
             dealt = y_banks[i][:].rearrange("j (p t) -> j t p", t=PACK)

from contextlib import ExitStack

import concourse.mybir as mybir
from concourse.masks import make_identity

K, T, S, N = 512, 1024, 512, 512
FLOPS = 2 * K * S * N

F32 = mybir.dt.float32
BF16 = mybir.dt.bfloat16
I32 = mybir.dt.int32
U32 = mybir.dt.uint32
U16 = mybir.dt.uint16
U8 = mybir.dt.uint8
FP8X4 = mybir.dt.float8_e4m3fn_x4
MULT = mybir.AluOpType.mult
ADD = mybir.AluOpType.add
COPY = mybir.ActivationFunctionType.Copy
IDENTITY = mybir.ActivationFunctionType.Identity

P = 128
PACK = 4
TILES = S // P
HALF = N // 2


def weave(copy, dst, src):
    copy(
        out=dst.rearrange("p (c i) t -> p c t i", i=4),
        in_=src.rearrange("p t (c i) -> p c t i", i=4),
    )


def quantize(nc, codes, scales, woven):
    nc.vector.quantize_mx(out=codes.bitcast(FP8X4), scales=scales, in_=woven.rearrange("p c t -> p (c t)"))


def tile_picked_lnfold_none_lo_kernel(tc, xT, mean, inv, gsum, b, w1, offs, out_0, out_1, out_2):
    nc = tc.nc
    with ExitStack() as ctx:
        sb = ctx.enter_context(tc.tile_pool(name="sb", bufs=1))
        ps = ctx.enter_context(tc.psum_pool(name="ps", bufs=1))

        lists = sb.tile([P, S // 16], U16, name="lists")
        nc.sync.dma_start(lists[:], offs)
        stats = sb.tile([P, T], F32, name="stats")
        nc.scalar.dma_start(out=stats[0:16, :], in_=mean[0:16, :])
        nc.sync.dma_start(out=stats[16:32, :], in_=inv[0:16, :])
        nc.gpsimd.memset(stats[64:128, 0:128], 0.0)
        nc.gpsimd.memset(stats[64:128, 128:896], 0.0)
        nc.vector.memset(stats[32:64, :], 0.0)
        nc.scalar.copy(out=stats[64:128, 896:1024], in_=stats[64:128, 0:128])
        g_col = sb.tile([P, PACK], F32, name="g_col")
        b_col = sb.tile([P, PACK], F32, name="b_col")
        nc.scalar.dma_start(out=g_col[:], in_=gsum.rearrange("(p t) o -> p (t o)", t=PACK))
        w_rows = w1.rearrange("(p t) m -> p t m", t=PACK)
        w_raw = [sb.tile([P, PACK, HALF], F32, name=f"w_raw{h}") for h in range(2)]
        nc.sync.dma_start(out=w_raw[0][:], in_=w_rows[:, :, 0:HALF])
        nc.sync.dma_start(out=w_raw[1][:], in_=w_rows[:, :, HALF:N])
        x_rows = xT.rearrange("(p t) c -> p t c", t=PACK)
        x_raw = [sb.tile([P, T], F32, name=f"x_raw{t}") for t in range(PACK)]
        for t in range(PACK):
            nc.sync.dma_start(out=x_raw[t][:], in_=x_rows[:, t, :])
        nc.sync.dma_start(out=b_col[:], in_=b.rearrange("(p t) o -> p (t o)", t=PACK))
        ident = sb.tile([P, P], F32, name="ident")
        make_identity(nc, ident[:])

        x_planes = sb.tile([P, PACK * S], BF16, name="x_planes", align_bytes=64)
        x_picked = x_planes[:].rearrange("p (t c) -> p t c", t=PACK)
        picked = sb.tile([P, S], F32, name="picked")
        nc.vector.tensor_copy(out=picked[:], in_=stats[:].indirect(lists[:]))

        g_bank = ps.tile([P, PACK, P], F32, name="g_bank", tag="y0")
        for t in range(PACK):
            nc.tensor.transpose(g_bank[:, t, :], g_col[:, t : t + 1].to_broadcast([P, P]), ident[:])
        stat_bank = ps.tile([P, TILES, P], F32, name="stat_bank", tag="y1")
        for i in range(TILES):
            nc.tensor.transpose(stat_bank[:, i, :], picked[:, i * P : (i + 1) * P], ident[:])

        g_rows = x_planes[:, 2 * S : 4 * S].bitcast(F32)
        nc.vector.tensor_copy(out=g_rows, in_=g_bank[:].rearrange("p t m -> p (t m)"))
        inv_col = sb.tile([P, TILES], F32, name="inv_col")
        nc.vector.tensor_copy(out=inv_col[:], in_=stat_bank[:, :, 16])
        shift_col = sb.tile([P, TILES], F32, name="shift_col")
        nc.vector.scalar_tensor_tensor(
            out=shift_col[:], in0=stat_bank[:, :, 0], scalar=-1.0, in1=inv_col[:], op0=MULT, op1=MULT
        )

        w_codes = sb.tile([P, N], U32, name="w_codes", align_bytes=64)
        w_scales = sb.tile([P, N], U8, name="w_scales", align_bytes=64)
        for h in range(2):
            cols = slice(h * HALF, (h + 1) * HALF)
            w_woven = sb.tile([P, HALF, PACK], BF16, name=f"w_woven{h}", tag=f"shift{2 + h}", align_bytes=64)
            weave(nc.scalar.copy, w_woven[:], w_raw[h][:])
            quantize(nc, w_codes[:, cols], w_scales[:, cols], w_woven[:])

        out_banks = [[ps.tile([P, 2, 2 * P], F32, name=f"out_bank{u}{v}") for v in range(2)] for u in range(2)]

        def out_block(i, t):
            return out_banks[i // 2][t // 2][:, t % 2, (i % 2) * P : (i % 2 + 1) * P]

        for i in range(TILES):
            shift = sb.tile([P, PACK, P], F32, name=f"shift{i}", align_bytes=64)
            nc.vector.tensor_scalar_mul(shift[:].rearrange("p t m -> p (t m)"), g_rows, shift_col[:, i : i + 1])
            for t in range(PACK):
                nc.tensor.matmul(
                    out_block(i, t), lhsT=shift[:, t, :], rhs=ident[:], is_transpose=True,
                    start=(i % 2 == 0 and t % 2 == 0), stop=False,
                )

        for t in range(2):
            nc.scalar.activation(out=x_picked[:, t, :], in_=x_raw[t][:].indirect(lists[:]), func=COPY)
        nc.vector.tensor_copy(out=x_picked[:, 2, :], in_=x_raw[2][:].indirect(lists[:]))
        nc.vector.tensor_copy(out=x_picked[:, 3, 0:P], in_=x_raw[3][:].indirect(lists[:, 0:8]))
        for i in range(1, TILES):
            nc.scalar.activation(
                out=x_picked[:, 3, i * P : (i + 1) * P], in_=x_raw[3][:].indirect(lists[:, 8 * i : 8 * i + 8]), func=COPY
            )

        x_woven = sb.tile([P, S, PACK], BF16, name="x_woven", align_bytes=64)
        x_codes = sb.tile([P, S], U32, name="x_codes", align_bytes=64)
        x_scales = sb.tile([P, S], U8, name="x_scales", align_bytes=64)
        for u in range(2):
            for i in (2 * u, 2 * u + 1):
                toks = slice(i * P, (i + 1) * P)
                copy = nc.scalar.copy if i == TILES - 1 else nc.vector.tensor_copy
                weave(copy, x_woven[:, toks, :], x_picked[:, :, toks])
            for i in (2 * u, 2 * u + 1):
                toks = slice(i * P, (i + 1) * P)
                quantize(nc, x_codes[:, toks], x_scales[:, toks], x_woven[:, toks, :])

        y_banks = [ps.tile([P, N], F32, name=f"y_bank{i}", tag=f"y{i}") for i in range(TILES)]
        for i in range(TILES):
            toks = slice(i * P, (i + 1) * P)
            nc.tensor.matmul_mx(
                out=y_banks[i][:],
                lhsT=x_codes[:, toks].bitcast(FP8X4),
                lhsT_scale=x_scales[:, toks],
                rhs=w_codes[:].bitcast(FP8X4),
                rhs_scale=w_scales[:],
                start=True,
                stop=True,
            )
        scaled = [sb.tile([P, PACK, P], F32, name=f"scaled{i}") for i in range(TILES)]
        for i in range(TILES):
            dealt = y_banks[i][:].rearrange("j (p t) -> j t p", t=PACK)
            if i % 2 == 0:
                nc.scalar.activation(out=scaled[i][:], in_=dealt, func=COPY, scale=inv_col[:, i : i + 1])
            else:
                nc.vector.tensor_scalar_mul(scaled[i][:], dealt, inv_col[:, i : i + 1])

        out_rows = out_0.rearrange("(p t) j -> p t j", t=PACK)
        out_words = out_1[0].rearrange("p j r -> p (j r)").bitcast(I32)
        o_woven = sb.tile([P, S, PACK], BF16, name="o_woven", align_bytes=64)
        o_codes = sb.tile([P, S], U32, name="o_codes", align_bytes=64)
        o_scales = sb.tile([P, S], U8, name="o_scales", align_bytes=64)
        for u in range(2):
            pair = slice(u * 2 * P, (u + 1) * 2 * P)
            for i in (2 * u, 2 * u + 1):
                for t in range(PACK):
                    nc.tensor.matmul(
                        out_block(i, t), lhsT=scaled[i][:, t, :], rhs=ident[:], is_transpose=True,
                        start=False, stop=(i % 2 == 1 and t % 2 == 1),
                    )
            result = sb.tile([P, PACK, 2 * P], F32, name=f"result{u}")
            for t in range(PACK):
                bank = out_banks[u][t // 2][:, t % 2, :]
                if t < 2:
                    nc.scalar.activation(out=result[:, t, :], in_=bank, func=IDENTITY, bias=b_col[:, t : t + 1])
                else:
                    nc.vector.tensor_scalar_add(result[:, t, :], bank, b_col[:, t : t + 1])
            for v in range(2):
                nc.sync.dma_start(out=out_rows[:, 2 * v : 2 * v + 2, pair], in_=result[:, 2 * v : 2 * v + 2, :])
            woven = o_woven[:, pair, :]
            weave(nc.vector.tensor_copy, woven[:, 0:160, :], result[:, :, 0:160])
            weave(nc.scalar.copy, woven[:, 160:256, :], result[:, :, 160:256])
            quantize(nc, o_codes[:, pair], o_scales[:, pair], woven)
            nc.sync.dma_start(out=out_words[:, pair], in_=o_codes[:, pair].bitcast(I32))
        scale_rows = out_2[0].bitcast(I32)
        for q in range(4):
            queue = nc.scalar if q % 2 else nc.sync
            queue.dma_start(out=scale_rows[4 * q : 4 * q + 4, :], in_=o_scales[32 * q : 32 * q + 4, :].bitcast(I32))
